import numpy as np
import ml_dtypes


def mxq(x, axis, fmt="e4m3"):
    dtype, down = {"e4m3": (ml_dtypes.float8_e4m3fn, 7), "e5m2": (ml_dtypes.float8_e5m2, 14)}[fmt]
    v = np.moveaxis(np.asarray(x, np.float32).astype(ml_dtypes.bfloat16).astype(np.float64), axis, -1)
    blocks = v.reshape(v.shape[:-1] + (-1, 32))
    amax = np.abs(blocks).max(-1, keepdims=True)
    byte = np.maximum(np.where(amax > 0, np.frexp(amax)[1] - 1 + 127, 0) - down, 1)
    scale = np.exp2(byte - 127.0)
    codes = (blocks / scale).astype(np.float32).astype(dtype).astype(np.float64)
    return np.moveaxis((codes * scale).reshape(v.shape), -1, axis)


WIDE = False


def mx_kscale(k):
    if not WIDE:
        return np.ones(k)
    levels = np.array([10, -10, 5, -5, 0])
    if k % 512:
        return np.exp2(np.random.permutation(np.resize(levels, k // 32))).repeat(32)
    a = np.empty((k // 512, 16))
    for p in range(k // 512):
        a[p, :8] = np.random.permutation(np.resize(levels, 8))
        for g in range(8):
            far = levels[np.abs(levels - a[p, g]) >= 10]
            a[p, g + 8] = far[np.random.randint(len(far))]
    return np.exp2(a.ravel()).repeat(32)


def f64(x):
    return np.asarray(x).astype(np.float64)


def striped(idx):
    return np.tile(idx.reshape(-1, 16).T, (8, 1)).astype(np.uint16)


def unstriped(offs):
    return offs[:16].T.reshape(-1).astype(np.int64)


E2M1 = np.array([0.0, 0.5, 1.0, 1.5, 2.0, 3.0, 4.0, 6.0, -0.0, -0.5, -1.0, -1.5, -2.0, -3.0, -4.0, -6.0])


def pack_weight(w, fmt):
    k, n = w.shape
    w = f64(np.asarray(w, np.float32).astype(ml_dtypes.bfloat16)).reshape(k // 32, 32, n)
    amax = np.abs(w).max(1)
    if fmt == "e4m3":
        byte = np.frexp(amax)[1] - 1 + 127 - 7
    else:
        mant, ex = np.frexp(amax / 6.0)
        byte = np.where(mant > 0.5, ex, ex - 1) + 127
    byte = np.clip(np.where(amax > 0, byte, 1), 1, 254)
    scaled = (w * np.exp2(127.0 - byte)[:, None, :]).reshape(k, n).astype(np.float32)
    by_word = np.ascontiguousarray(scaled.reshape(k // 512, 128, 4, n).transpose(0, 1, 3, 2))
    if fmt == "e4m3":
        words = by_word.astype(ml_dtypes.float8_e4m3fn).view(np.uint8)
    else:
        c = by_word.astype(ml_dtypes.float4_e2m1fn).view(np.uint8) & 0xF
        words = (c[..., 0::2] | (c[..., 1::2] << 4)).reshape(k // 512, 128, 2 * n)
    return np.ascontiguousarray(words), np.ascontiguousarray(byte.astype(np.uint8).reshape(k // 512, 16, n))


def unpack_weight(words, scales, fmt):
    g, _, n = scales.shape
    words = np.ascontiguousarray(words).reshape(g, 128, n, -1)
    if fmt == "e4m3":
        vals = words.view(ml_dtypes.float8_e4m3fn).astype(np.float64)
    else:
        nib = np.empty((g, 128, n, 4), np.uint8)
        nib[..., 0::2] = words & 0xF
        nib[..., 1::2] = words >> 4
        vals = E2M1[nib]
    vals = vals * np.repeat(np.exp2(scales.astype(np.float64) - 127.0), 8, axis=1)[..., None]
    return vals.transpose(0, 1, 3, 2).reshape(g * 512, n)


def gelu(v):
    return 0.5 * v * (1.0 + np.tanh(np.sqrt(2.0 / np.pi) * (v + 0.044715 * v**3)))


def striped8(idx):
    return np.concatenate([v.reshape(-1, 16).T for v in idx]).astype(np.uint16)


def unstriped8(offs):
    return np.stack([offs[16 * g:16 * g + 16].T.reshape(-1) for g in range(8)]).astype(np.int64)


def put_heads(h, wgs, idx8, t2):
    r = np.arange(h.shape[0])
    page = np.zeros((h.shape[0], t2))
    page[r[:, None], idx8[r % 512 // 64]] = wgs[r // 4 % 128] * h
    return page


K, T, S, H, T2, P, N = 1024, 4096, 1024, 1024, 2048, 1024, 512

def setup_inputs():
    n = np.random.standard_normal
    s = mx_kscale(K)[:, None]
    u = mx_kscale(H)[:, None]
    tab_words, tab_scales = pack_weight(n((K, T)) * s, "e4m3")
    w2_words, w2_scales = pack_weight(n((H, N)) / np.sqrt(H) / u, "e2m1")
    idx8 = np.stack([np.random.permutation(T2)[:S] for _ in range(8)])
    return {
        "tab_words": tab_words, "tab_scales": tab_scales,
        "offs": striped(np.random.permutation(T)[:S]),
        "w1": (0.5 * n((K, H)) / np.sqrt(K) / s).astype(np.float32),
        "gain": (3.0 * np.exp(0.3 * n(H)) * u[:, 0]).astype(np.float32),
        "wgs": np.repeat(np.random.uniform(0.5, 2.0, (8, S)), 16, axis=0).astype(np.float32),
        "offs2": striped8(idx8),
        "offs3": striped(np.random.permutation(T2)[:P]),
        "ref": (n((H, P)) * u).astype(np.float32),
        "w2_words": w2_words, "w2_scales": w2_scales,
        "wm": np.exp(0.4 * n((N, P))).astype(np.float32),
    }

def reference(tab_words, tab_scales, offs, w1, gain, wgs, offs2, offs3, ref, w2_words, w2_scales, wm):
    v = unpack_weight(tab_words, tab_scales, "e4m3")[:, unstriped(offs)]
    w1q = mxq(f64(w1), 0, "e4m3")
    f = w1q.T @ v
    h = f64(gain)[:, None] * (f * np.cos(f))
    page = put_heads(h, f64(wgs), unstriped8(offs2), T2)
    x = page[:, unstriped(offs3)]
    z = np.maximum(x, f64(ref))
    zq = mxq(z, 0, "e4m3")
    w2 = unpack_weight(w2_words, w2_scales, "e2m1")
    y = w2.T @ zq
    return f64(wm) * y

@@ -1,0 +1,297 @@
+import math
+from contextlib import ExitStack
+
+import concourse.mybir as mybir
+
+K, T, S, H, T2, M, N = 1024, 4096, 1024, 1024, 2048, 1024, 512
+FLOPS = 2 * K * H * S + 2 * H * N * M
+
+F32 = mybir.dt.float32
+BF16 = mybir.dt.bfloat16
+I32 = mybir.dt.int32
+U32 = mybir.dt.uint32
+U16 = mybir.dt.uint16
+U8 = mybir.dt.uint8
+FP8X4 = mybir.dt.float8_e4m3fn_x4
+FP4X4 = mybir.dt.float4_e2m1fn_x4
+ACT = mybir.ActivationFunctionType
+ALU = mybir.AluOpType
+
+P = 128
+PACK = 4
+PASS = P * PACK
+BANK = 512
+BANKS = 8
+GROUP = 16
+CHUNK = 256
+CHUNKS = M // CHUNK
+SLICES = H // P
+
+
+def tile_list_beam_slot_calibration_kernel(
+    tc, tab_words, tab_scales, offs, w1, gain, wgs, offs2, offs3, ref, w2_words, w2_scales, wm, out
+):
+    nc = tc.nc
+    with ExitStack() as ctx:
+        held = ctx.enter_context(tc.tile_pool(name="held", bufs=1))
+        ring = ctx.enter_context(tc.tile_pool(name="ring", bufs=2))
+        psum = ctx.enter_context(tc.psum_pool(name="psum", bufs=1))
+
+        def entries(offsets, j0, n):
+            return offsets[:, j0 // GROUP : (j0 + n) // GROUP]
+
+        banks_taken = []
+
+        def next_bank(shape):
+            name = "bank%d" % (len(banks_taken) % BANKS)
+            bank = psum.tile(shape, F32, name=name, tag=name)
+            banks_taken.append(name)
+            return bank
+
+        tab_planes = held.tile([P, T], U8, name="tab_planes", align_bytes=64)
+        nc.vector.memset(tab_planes[:].bitcast(I32), 0)
+        w2_planes = held.tile([P, 2 * N], U8, name="w2_planes", align_bytes=64)
+        nc.vector.memset(w2_planes[:].bitcast(I32), 0)
+
+        page = held.tile([P, T2], F32, name="page")
+        nc.vector.memset(page[:], 0.0)
+
+        idx = held.tile([P, S // GROUP], U16, name="idx")
+        nc.sync.dma_start(idx[:], offs)
+
+        def load_table(a):
+            words = held.tile([P, T], U32, name="tab%d" % a, align_bytes=64)
+            nc.sync.dma_start(
+                out=words[:].bitcast(I32), in_=tab_words[a].rearrange("p t i -> p (t i)").bitcast(I32)
+            )
+            return words
+
+        def load_w1(a, b):
+            raw = held.tile([P, PACK, PASS], F32, name="w1_raw%d%d" % (a, b))
+            rows = w1[a * PASS : (a + 1) * PASS, b * PASS : (b + 1) * PASS]
+            nc.sync.dma_start(out=raw[:], in_=rows.rearrange("(p j) c -> p j c", j=PACK))
+            return raw
+
+        def load_ref(s):
+            rows = held.tile([P, M], F32, name="ref%d" % s)
+            nc.sync.dma_start(out=rows[:], in_=ref.rearrange("(b p i) m -> b i p m", b=2, i=PACK)[s // PACK, s % PACK])
+            return rows
+
+        table = [load_table(0)]
+        for q in range(4):
+            nc.sync.dma_start(
+                out=tab_planes[32 * q : 32 * q + 8, :].bitcast(I32),
+                in_=tab_scales[:, 4 * q : 4 * q + 4, :].bitcast(I32),
+            )
+        w1_raw = {(a, 0): load_w1(a, 0) for a in range(2)}
+        gains = held.tile([P, 2, PACK], F32, name="gains")
+        nc.sync.dma_start(out=gains[:], in_=gain.rearrange("(b p i) -> p b i", b=2, i=PACK))
+        idx2 = held.tile([P, S // GROUP], U16, name="idx2")
+        nc.sync.dma_start(idx2[:], offs2)
+        table.append(load_table(1))
+        slot_w = held.tile([P, S], F32, name="slot_w")
+        nc.sync.dma_start(out=slot_w[:], in_=wgs)
+        idx3 = held.tile([P, M // GROUP], U16, name="idx3")
+        nc.sync.dma_start(idx3[:], offs3)
+        refs = [load_ref(0)]
+        for a in range(2):
+            w1_raw[a, 1] = load_w1(a, 1)
+        refs.extend([load_ref(s) for s in range(1, SLICES)])
+        w2_codes = held.tile([P, 2, 2 * N], U8, name="w2_codes", align_bytes=64)
+        nc.sync.dma_start(out=w2_codes[:].bitcast(I32), in_=w2_words.bitcast(I32).rearrange("b p c -> p b c"))
+        for q in range(4):
+            nc.sync.dma_start(
+                out=w2_planes[32 * q : 32 * q + 4, :].bitcast(I32).rearrange("r (b c) -> r b c", b=2),
+                in_=w2_scales[:, 4 * q : 4 * q + 4, :].bitcast(I32).rearrange("b r c -> r b c"),
+            )
+        out_w = []
+        for c in range(CHUNKS):
+            cols = held.tile([P, N // P, CHUNK], F32, name="out_w%d" % c)
+            nc.sync.dma_start(
+                out=cols[:], in_=wm[:, c * CHUNK : (c + 1) * CHUNK].rearrange("(t p) m -> p t m", p=P)
+            )
+            out_w.append(cols)
+
+        picked = {}
+
+        def pick_words(a, half):
+            words = held.tile([P, BANK], U32, name="picked%d%d" % (a, half), align_bytes=64)
+            nc.vector.tensor_copy(words[:], table[a][:].indirect(entries(idx, half * BANK, BANK)))
+            picked[a, half] = words
+
+        w1_round, w1_codes, w1_planes = {}, {}, {}
+
+        def round_w1(a, b, copy):
+            grouped = ring.tile([P, PACK, P, PACK], BF16, name="w1_grouped", align_bytes=64)
+            copy(
+                out=grouped[:].rearrange("p t m j -> p m j t"),
+                in_=w1_raw[a, b][:].rearrange("p j (m t) -> p m j t", t=PACK),
+            )
+            w1_round[a, b] = grouped
+
+        def quantize_w1(a, b):
+            w1_codes[a, b] = held.tile([P, PASS], U32, name="w1_codes%d%d" % (a, b), align_bytes=64)
+            w1_planes[a, b] = held.tile([P, PASS], U8, name="w1_planes%d%d" % (a, b), align_bytes=64)
+            nc.vector.quantize_mx(
+                out=w1_codes[a, b][:].bitcast(FP8X4),
+                scales=w1_planes[a, b][:],
+                in_=w1_round[a, b][:].rearrange("p t m j -> p (t m j)"),
+            )
+
+        pick_words(0, 0)
+        pick_words(0, 1)
+        picked_planes = held.tile([P, S], U8, name="picked_planes", align_bytes=64)
+        nc.vector.tensor_copy(picked_planes[:], tab_planes[:].indirect(idx[:]))
+        round_w1(0, 0, nc.vector.tensor_copy)
+        round_w1(1, 0, nc.vector.tensor_copy)
+        quantize_w1(0, 0)
+        quantize_w1(1, 0)
+        pick_words(1, 0)
+        pick_words(1, 1)
+
+        def pieces(s):
+            if s == 0:
+                return [(0, 256), (256, 256), (512, 512)]
+            return [(0, BANK), (BANK, BANK)]
+
+        features = {}
+
+        def feature(s):
+            b, i = divmod(s, PACK)
+            rows = slice(i * P, (i + 1) * P)
+            for j0, n in pieces(s):
+                f = next_bank([P, n])
+                half, c0 = divmod(j0, BANK)
+                for a in range(2):
+                    nc.tensor.matmul_mx(
+                        out=f[:],
+                        lhsT=w1_codes[a, b][:, rows].bitcast(FP8X4),
+                        lhsT_scale=w1_planes[a, b][:, rows],
+                        rhs=picked[a, half][:, c0 : c0 + n].bitcast(FP8X4),
+                        rhs_scale=picked_planes[4 * a : P, j0 : j0 + n],
+                        start=(a == 0),
+                        stop=(a == 1),
+                    )
+                size = ring.tile([P, n], F32, name="size")
+                nc.scalar.activation(size[:], f[:], ACT.Abs)
+                cos = ring.tile([P, n], F32, name="cos", bufs=6)
+                nc.scalar.activation(cos[:], size[:], ACT.Sin, scale=-1.0, bias=math.pi / 2)
+                features[s, j0] = (f, cos)
+
+        h_tiles = {}
+
+        def product(s, piece):
+            b, i = divmod(s, PACK)
+            j0, n = pieces(s)[piece]
+            if piece == 0:
+                h_tiles[s] = ring.tile([P, S], F32, name="h")
+            f, cos = features[s, j0]
+            nc.vector.scalar_tensor_tensor(
+                h_tiles[s][:, j0 : j0 + n], f[:], gains[:, b, i : i + 1], cos[:], ALU.mult, ALU.mult
+            )
+
+        def scatter(s, j0, n):
+            nc.vector.tensor_tensor(
+                page[:].indirect(entries(idx2, j0, n)), h_tiles[s][:, j0 : j0 + n], slot_w[:, j0 : j0 + n], ALU.mult
+            )
+
+        x_tiles = {}
+
+        def gather(s, m0, n):
+            if m0 == 0:
+                x_tiles[s] = ring.tile([P, M], F32, name="x", bufs=1)
+            nc.vector.tensor_copy(x_tiles[s][:, m0 : m0 + n], page[:].indirect(entries(idx3, m0, n)))
+
+        z_rows = [held.tile([P, CHUNKS, PACK, CHUNK], BF16, name="z_rows%d" % b) for b in range(2)]
+
+        def floor_at_ref(s, c0, c1):
+            b, i = divmod(s, PACK)
+            cols = slice(c0 * CHUNK, c1 * CHUNK)
+            nc.vector.tensor_tensor(
+                z_rows[b][:, c0:c1, i, :],
+                x_tiles[s][:, cols].rearrange("p (c m) -> p c m", m=CHUNK),
+                refs[s][:, cols].rearrange("p (c m) -> p c m", m=CHUNK),
+                ALU.max,
+            )
+
+        z_woven, z_codes, z_planes = {}, {}, {}
+
+        def weave(b, c):
+            woven = ring.tile([P, CHUNK, PACK], BF16, name="z_woven", align_bytes=64, bufs=4)
+            nc.scalar.copy(
+                out=woven[:].rearrange("p (g e) t -> p g t e", e=4),
+                in_=z_rows[b][:, c, :, :].rearrange("p t (g e) -> p g t e", e=4),
+            )
+            z_woven[b, c] = woven
+
+        def quantize_z(b, c):
+            z_codes[b, c] = held.tile([P, CHUNK], U32, name="z_codes%d%d" % (b, c), align_bytes=64)
+            z_planes[b, c] = held.tile([P, CHUNK], U8, name="z_planes%d%d" % (b, c), align_bytes=64)
+            nc.vector.quantize_mx(
+                out=z_codes[b, c][:].bitcast(FP8X4),
+                scales=z_planes[b, c][:],
+                in_=z_woven[b, c][:].rearrange("p m t -> p (m t)"),
+            )
+
+        y_banks = {}
+
+        def calibrate(b, c):
+            for pair in range(2):
+                if b == 0:
+                    y_banks[c, pair] = next_bank([P, 2, CHUNK])
+                for u in range(2):
+                    t = 2 * pair + u
+                    nc.tensor.matmul_mx(
+                        out=y_banks[c, pair][:, u, :],
+                        lhsT=w2_codes[:, b, 2 * P * t : 2 * P * (t + 1)].bitcast(FP4X4),
+                        lhsT_scale=w2_planes[:, b * N + P * t : b * N + P * (t + 1)],
+                        rhs=z_codes[b, c][:].bitcast(FP8X4),
+                        rhs_scale=z_planes[b, c][:],
+                        start=(b == 0 and u == 0),
+                        stop=(b == 1 and u == 1),
+                    )
+
+        def weigh(c):
+            for pair in range(2):
+                both = out_w[c][:, 2 * pair : 2 * pair + 2, :]
+                nc.vector.tensor_tensor(both, y_banks[c, pair][:], both, ALU.mult)
+                rows = out[2 * P * pair : 2 * P * (pair + 1), c * CHUNK : (c + 1) * CHUNK]
+                nc.sync.dma_start(out=rows.rearrange("(u p) m -> p u m", p=P), in_=both)
+
+        feature(0)
+        feature(1)
+        for piece, (j0, n) in enumerate(pieces(0)):
+            product(0, piece)
+            scatter(0, j0, n)
+        last = SLICES - 1
+        for s in range(last):
+            if s + 2 < SLICES:
+                feature(s + 2)
+            if s < 2:
+                round_w1(s, 1, nc.scalar.copy)
+            product(s + 1, 0)
+            gather(s, 0, M)
+            product(s + 1, 1)
+            floor_at_ref(s, 0, CHUNKS)
+            if s < 2:
+                quantize_w1(s, 1)
+            if s == PACK - 1:
+                for c in range(CHUNKS):
+                    weave(0, c)
+            if s >= PACK:
+                for c in range(2 * (s - PACK), min(2 * (s - PACK) + 2, CHUNKS)):
+                    quantize_z(0, c)
+            scatter(s + 1, 0, S)
+        for c in range(CHUNKS):
+            calibrate(0, c)
+        for step in range(CHUNKS + 3):
+            if step < CHUNKS:
+                gather(last, step * CHUNK, CHUNK)
+            if 0 <= step - 1 < CHUNKS:
+                floor_at_ref(last, step - 1, step)
+                weave(1, step - 1)
+            if 0 <= step - 2 < CHUNKS:
+                quantize_z(1, step - 2)
+                calibrate(1, step - 2)
+            if 0 <= step - 3 < CHUNKS:
+                weigh(step - 3)

@@ -56,8 +56,6 @@ def tile_list_beam_slot_calibration_kernel(
         page = held.tile([P, T2], F32, name="page")
         nc.vector.memset(page[:], 0.0)
 
-        idx = held.tile([P, S // GROUP], U16, name="idx")
-        nc.sync.dma_start(idx[:], offs)
 
         def load_table(a):
             words = held.tile([P, T], U32, name="tab%d" % a, align_bytes=64)
@@ -78,6 +76,8 @@ def tile_list_beam_slot_calibration_kernel(
             return rows
 
         table = [load_table(0)]
+        idx = held.tile([P, S // GROUP], U16, name="idx")
+        nc.sync.dma_start(idx[:], offs)
         for q in range(4):
             nc.sync.dma_start(
                 out=tab_planes[32 * q : 32 * q + 8, :].bitcast(I32),
@@ -122,20 +122,21 @@ def tile_list_beam_slot_calibration_kernel(
         w1_round, w1_codes, w1_planes = {}, {}, {}
 
         def round_w1(a, b, copy):
-            grouped = ring.tile([P, PACK, P, PACK], BF16, name="w1_grouped", align_bytes=64)
+            if a == 0:
+                w1_round[b] = held.tile([P, 2 * PACK * PASS], BF16, name="w1_round", align_bytes=64)
+                w1_codes[b] = held.tile([P, 2 * PASS], U32, name="w1_codes%d" % b, align_bytes=64)
+                w1_planes[b] = held.tile([P, 2 * PASS], U8, name="w1_planes%d" % b, align_bytes=64)
+            grouped = w1_round[b][:, a * PACK * PASS : (a + 1) * PACK * PASS]
             copy(
-                out=grouped[:].rearrange("p t m j -> p m j t"),
+                out=grouped.rearrange("p (t m j) -> p m j t", t=PACK, j=PACK),
                 in_=w1_raw[a, b][:].rearrange("p j (m t) -> p m j t", t=PACK),
             )
-            w1_round[a, b] = grouped
 
-        def quantize_w1(a, b):
-            w1_codes[a, b] = held.tile([P, PASS], U32, name="w1_codes%d%d" % (a, b), align_bytes=64)
-            w1_planes[a, b] = held.tile([P, PASS], U8, name="w1_planes%d%d" % (a, b), align_bytes=64)
+        def quantize_w1(b, a0, a1):
             nc.vector.quantize_mx(
-                out=w1_codes[a, b][:].bitcast(FP8X4),
-                scales=w1_planes[a, b][:],
-                in_=w1_round[a, b][:].rearrange("p t m j -> p (t m j)"),
+                out=w1_codes[b][:, a0 * PASS : a1 * PASS].bitcast(FP8X4),
+                scales=w1_planes[b][:, a0 * PASS : a1 * PASS],
+                in_=w1_round[b][:, a0 * PACK * PASS : a1 * PACK * PASS],
             )
 
         pick_words(0, 0)
@@ -144,8 +145,8 @@ def tile_list_beam_slot_calibration_kernel(
         nc.vector.tensor_copy(picked_planes[:], tab_planes[:].indirect(idx[:]))
         round_w1(0, 0, nc.vector.tensor_copy)
         round_w1(1, 0, nc.vector.tensor_copy)
-        quantize_w1(0, 0)
-        quantize_w1(1, 0)
+        quantize_w1(0, 0, 1)
+        quantize_w1(0, 1, 2)
         pick_words(1, 0)
         pick_words(1, 1)
 
@@ -154,19 +155,22 @@ def tile_list_beam_slot_calibration_kernel(
                 return [(0, 256), (256, 256), (512, 512)]
             return [(0, BANK), (BANK, BANK)]
 
-        features = {}
+        banks_f, cosines, scaled = {}, {}, {}
 
         def feature(s):
             b, i = divmod(s, PACK)
-            rows = slice(i * P, (i + 1) * P)
+            cosines[s] = ring.tile([P, S], F32, name="cosine")
+            if s > 0:
+                scaled[s] = ring.tile([P, S], F32, name="scaled")
             for j0, n in pieces(s):
                 f = next_bank([P, n])
                 half, c0 = divmod(j0, BANK)
                 for a in range(2):
+                    rows = slice(a * PASS + i * P, a * PASS + (i + 1) * P)
                     nc.tensor.matmul_mx(
                         out=f[:],
-                        lhsT=w1_codes[a, b][:, rows].bitcast(FP8X4),
-                        lhsT_scale=w1_planes[a, b][:, rows],
+                        lhsT=w1_codes[b][:, rows].bitcast(FP8X4),
+                        lhsT_scale=w1_planes[b][:, rows],
                         rhs=picked[a, half][:, c0 : c0 + n].bitcast(FP8X4),
                         rhs_scale=picked_planes[4 * a : P, j0 : j0 + n],
                         start=(a == 0),
@@ -174,32 +178,48 @@ def tile_list_beam_slot_calibration_kernel(
                     )
                 size = ring.tile([P, n], F32, name="size")
                 nc.scalar.activation(size[:], f[:], ACT.Abs)
-                cos = ring.tile([P, n], F32, name="cos", bufs=6)
-                nc.scalar.activation(cos[:], size[:], ACT.Sin, scale=-1.0, bias=math.pi / 2)
-                features[s, j0] = (f, cos)
+                nc.scalar.activation(cosines[s][:, j0 : j0 + n], size[:], ACT.Sin, scale=-1.0, bias=math.pi / 2)
+                if s > 0:
+                    nc.scalar.activation(scaled[s][:, j0 : j0 + n], f[:], ACT.Copy, scale=gains[:, b, i : i + 1])
+                banks_f[s, j0] = f
 
-        h_tiles = {}
+        def stage(s, what):
+            return held.tile([P, S], F32, name="%s%d" % (what, s), tag="stage%d" % (s % 2))
 
-        def product(s, piece):
-            b, i = divmod(s, PACK)
-            j0, n = pieces(s)[piece]
-            if piece == 0:
-                h_tiles[s] = ring.tile([P, S], F32, name="h")
-            f, cos = features[s, j0]
-            nc.vector.scalar_tensor_tensor(
-                h_tiles[s][:, j0 : j0 + n], f[:], gains[:, b, i : i + 1], cos[:], ALU.mult, ALU.mult
-            )
+        weighted = {}
+
+        def products(s):
+            h = stage(s, "h")
+            nc.gpsimd.tensor_tensor(h[:], scaled[s][:], cosines[s][:], ALU.mult)
+            weighted[s] = ring.tile([P, S], F32, name="weighted")
+            nc.gpsimd.tensor_tensor(weighted[s][:], h[:], slot_w[:], ALU.mult)
 
         def scatter(s, j0, n):
-            nc.vector.tensor_tensor(
-                page[:].indirect(entries(idx2, j0, n)), h_tiles[s][:, j0 : j0 + n], slot_w[:, j0 : j0 + n], ALU.mult
-            )
+            nc.vector.tensor_copy(page[:].indirect(entries(idx2, j0, n)), weighted[s][:, j0 : j0 + n])
+
+        def first_slice():
+            h = stage(1, "first")
+            weighted[0] = ring.tile([P, S], F32, name="weighted")
+            head, rest = pieces(0)[0], pieces(0)[1:]
+            for j0, n in pieces(0):
+                cols = slice(j0, j0 + n)
+                nc.vector.scalar_tensor_tensor(
+                    h[:, cols], banks_f[0, j0][:], gains[:, 0, 0:1], cosines[0][:, cols], ALU.mult, ALU.mult
+                )
+                if (j0, n) == head:
+                    nc.vector.tensor_tensor(
+                        page[:].indirect(entries(idx2, j0, n)), h[:, cols], slot_w[:, cols], ALU.mult
+                    )
+            for j0, n in rest:
+                cols = slice(j0, j0 + n)
+                nc.vector.tensor_tensor(weighted[0][:, cols], h[:, cols], slot_w[:, cols], ALU.mult)
+            scatter(0, rest[0][0], S - rest[0][0])
 
         x_tiles = {}
 
         def gather(s, m0, n):
             if m0 == 0:
-                x_tiles[s] = ring.tile([P, M], F32, name="x", bufs=1)
+                x_tiles[s] = stage(s, "x")
             nc.vector.tensor_copy(x_tiles[s][:, m0 : m0 + n], page[:].indirect(entries(idx3, m0, n)))
 
         z_rows = [held.tile([P, CHUNKS, PACK, CHUNK], BF16, name="z_rows%d" % b) for b in range(2)]
@@ -217,20 +237,21 @@ def tile_list_beam_slot_calibration_kernel(
         z_woven, z_codes, z_planes = {}, {}, {}
 
         def weave(b, c):
-            woven = ring.tile([P, CHUNK, PACK], BF16, name="z_woven", align_bytes=64, bufs=4)
+            if c == 0:
+                z_woven[b] = held.tile([P, PACK * M], BF16, name="z_woven", align_bytes=64)
+                z_codes[b] = held.tile([P, M], U32, name="z_codes%d" % b, align_bytes=64)
+                z_planes[b] = held.tile([P, M], U8, name="z_planes%d" % b, align_bytes=64)
+            woven = z_woven[b][:, c * PACK * CHUNK : (c + 1) * PACK * CHUNK]
             nc.scalar.copy(
-                out=woven[:].rearrange("p (g e) t -> p g t e", e=4),
+                out=woven.rearrange("p (g e t) -> p g t e", e=4, t=PACK),
                 in_=z_rows[b][:, c, :, :].rearrange("p t (g e) -> p g t e", e=4),
             )
-            z_woven[b, c] = woven
 
-        def quantize_z(b, c):
-            z_codes[b, c] = held.tile([P, CHUNK], U32, name="z_codes%d%d" % (b, c), align_bytes=64)
-            z_planes[b, c] = held.tile([P, CHUNK], U8, name="z_planes%d%d" % (b, c), align_bytes=64)
+        def quantize_z(b, c0, c1):
             nc.vector.quantize_mx(
-                out=z_codes[b, c][:].bitcast(FP8X4),
-                scales=z_planes[b, c][:],
-                in_=z_woven[b, c][:].rearrange("p m t -> p (m t)"),
+                out=z_codes[b][:, c0 * CHUNK : c1 * CHUNK].bitcast(FP8X4),
+                scales=z_planes[b][:, c0 * CHUNK : c1 * CHUNK],
+                in_=z_woven[b][:, c0 * PACK * CHUNK : c1 * PACK * CHUNK],
             )
 
         y_banks = {}
@@ -245,8 +266,8 @@ def tile_list_beam_slot_calibration_kernel(
                         out=y_banks[c, pair][:, u, :],
                         lhsT=w2_codes[:, b, 2 * P * t : 2 * P * (t + 1)].bitcast(FP4X4),
                         lhsT_scale=w2_planes[:, b * N + P * t : b * N + P * (t + 1)],
-                        rhs=z_codes[b, c][:].bitcast(FP8X4),
-                        rhs_scale=z_planes[b, c][:],
+                        rhs=z_codes[b][:, c * CHUNK : (c + 1) * CHUNK].bitcast(FP8X4),
+                        rhs_scale=z_planes[b][:, c * CHUNK : (c + 1) * CHUNK],
                         start=(b == 0 and u == 0),
                         stop=(b == 1 and u == 1),
                     )
@@ -260,27 +281,25 @@ def tile_list_beam_slot_calibration_kernel(
 
         feature(0)
         feature(1)
-        for piece, (j0, n) in enumerate(pieces(0)):
-            product(0, piece)
-            scatter(0, j0, n)
+        first_slice()
         last = SLICES - 1
         for s in range(last):
+            products(s + 1)
             if s + 2 < SLICES:
                 feature(s + 2)
             if s < 2:
                 round_w1(s, 1, nc.scalar.copy)
-            product(s + 1, 0)
-            gather(s, 0, M)
-            product(s + 1, 1)
-            floor_at_ref(s, 0, CHUNKS)
-            if s < 2:
-                quantize_w1(s, 1)
+            for half in range(2):
+                gather(s, half * BANK, BANK)
+            for half in range(2):
+                floor_at_ref(s, 2 * half, 2 * half + 2)
+            if s == 1:
+                quantize_w1(1, 0, 2)
             if s == PACK - 1:
                 for c in range(CHUNKS):
                     weave(0, c)
-            if s >= PACK:
-                for c in range(2 * (s - PACK), min(2 * (s - PACK) + 2, CHUNKS)):
-                    quantize_z(0, c)
+            if s == PACK:
+                quantize_z(0, 0, CHUNKS)
             scatter(s + 1, 0, S)
         for c in range(CHUNKS):
             calibrate(0, c)
@@ -291,7 +310,7 @@ def tile_list_beam_slot_calibration_kernel(
                 floor_at_ref(last, step - 1, step)
                 weave(1, step - 1)
             if 0 <= step - 2 < CHUNKS:
-                quantize_z(1, step - 2)
+                quantize_z(1, step - 2, step - 1)
                 calibrate(1, step - 2)
             if 0 <= step - 3 < CHUNKS:
                 weigh(step - 3)

@@ -53,8 +53,9 @@ def tile_list_beam_slot_calibration_kernel(
         w2_planes = held.tile([P, 2 * N], U8, name="w2_planes", align_bytes=64)
         nc.vector.memset(w2_planes[:].bitcast(I32), 0)
 
-        page = held.tile([P, T2], F32, name="page")
-        nc.vector.memset(page[:], 0.0)
+        pages = [held.tile([P, T2], F32, name="page%d" % n) for n in range(2)]
+        for page in pages:
+            nc.vector.memset(page[:], 0.0)
 
 
         def load_table(a):
@@ -84,11 +85,11 @@ def tile_list_beam_slot_calibration_kernel(
                 in_=tab_scales[:, 4 * q : 4 * q + 4, :].bitcast(I32),
             )
         w1_raw = {(a, 0): load_w1(a, 0) for a in range(2)}
+        table.append(load_table(1))
         gains = held.tile([P, 2, PACK], F32, name="gains")
         nc.sync.dma_start(out=gains[:], in_=gain.rearrange("(b p i) -> p b i", b=2, i=PACK))
         idx2 = held.tile([P, S // GROUP], U16, name="idx2")
         nc.sync.dma_start(idx2[:], offs2)
-        table.append(load_table(1))
         slot_w = held.tile([P, S], F32, name="slot_w")
         nc.sync.dma_start(out=slot_w[:], in_=wgs)
         idx3 = held.tile([P, M // GROUP], U16, name="idx3")
@@ -128,8 +129,8 @@ def tile_list_beam_slot_calibration_kernel(
                 w1_planes[b] = held.tile([P, 2 * PASS], U8, name="w1_planes%d" % b, align_bytes=64)
             grouped = w1_round[b][:, a * PACK * PASS : (a + 1) * PACK * PASS]
             copy(
-                out=grouped.rearrange("p (t m j) -> p m j t", t=PACK, j=PACK),
-                in_=w1_raw[a, b][:].rearrange("p j (m t) -> p m j t", t=PACK),
+                out=grouped.rearrange("p (u e m j) -> p u m j e", u=2, e=2, j=PACK),
+                in_=w1_raw[a, b][:].rearrange("p j (m u e) -> p u m j e", u=2, e=2),
             )
 
         def quantize_w1(b, a0, a1):
@@ -143,7 +144,7 @@ def tile_list_beam_slot_calibration_kernel(
         pick_words(0, 1)
         picked_planes = held.tile([P, S], U8, name="picked_planes", align_bytes=64)
         nc.vector.tensor_copy(picked_planes[:], tab_planes[:].indirect(idx[:]))
-        round_w1(0, 0, nc.vector.tensor_copy)
+        round_w1(0, 0, nc.scalar.copy)
         round_w1(1, 0, nc.vector.tensor_copy)
         quantize_w1(0, 0, 1)
         quantize_w1(0, 1, 2)
@@ -183,19 +184,19 @@ def tile_list_beam_slot_calibration_kernel(
                     nc.scalar.activation(scaled[s][:, j0 : j0 + n], f[:], ACT.Copy, scale=gains[:, b, i : i + 1])
                 banks_f[s, j0] = f
 
-        def stage(s, what):
-            return held.tile([P, S], F32, name="%s%d" % (what, s), tag="stage%d" % (s % 2))
+        def stage(n, name):
+            return held.tile([P, S], F32, name=name, tag="stage%d" % (n % 2))
 
         weighted = {}
 
         def products(s):
-            h = stage(s, "h")
+            h = stage(s, "h%d" % s)
             nc.gpsimd.tensor_tensor(h[:], scaled[s][:], cosines[s][:], ALU.mult)
             weighted[s] = ring.tile([P, S], F32, name="weighted")
             nc.gpsimd.tensor_tensor(weighted[s][:], h[:], slot_w[:], ALU.mult)
 
         def scatter(s, j0, n):
-            nc.vector.tensor_copy(page[:].indirect(entries(idx2, j0, n)), weighted[s][:, j0 : j0 + n])
+            nc.vector.tensor_copy(pages[s % 2][:].indirect(entries(idx2, j0, n)), weighted[s][:, j0 : j0 + n])
 
         def first_slice():
             h = stage(1, "first")
@@ -208,7 +209,7 @@ def tile_list_beam_slot_calibration_kernel(
                 )
                 if (j0, n) == head:
                     nc.vector.tensor_tensor(
-                        page[:].indirect(entries(idx2, j0, n)), h[:, cols], slot_w[:, cols], ALU.mult
+                        pages[0][:].indirect(entries(idx2, j0, n)), h[:, cols], slot_w[:, cols], ALU.mult
                     )
             for j0, n in rest:
                 cols = slice(j0, j0 + n)
@@ -219,8 +220,8 @@ def tile_list_beam_slot_calibration_kernel(
 
         def gather(s, m0, n):
             if m0 == 0:
-                x_tiles[s] = stage(s, "x")
-            nc.vector.tensor_copy(x_tiles[s][:, m0 : m0 + n], page[:].indirect(entries(idx3, m0, n)))
+                x_tiles[s] = stage(s + 1 if s > 0 else 0, "x%d" % s)
+            nc.vector.tensor_copy(x_tiles[s][:, m0 : m0 + n], pages[s % 2][:].indirect(entries(idx3, m0, n)))
 
         z_rows = [held.tile([P, CHUNKS, PACK, CHUNK], BF16, name="z_rows%d" % b) for b in range(2)]
 
@@ -283,24 +284,31 @@ def tile_list_beam_slot_calibration_kernel(
         feature(1)
         first_slice()
         last = SLICES - 1
-        for s in range(last):
-            products(s + 1)
-            if s + 2 < SLICES:
-                feature(s + 2)
-            if s < 2:
-                round_w1(s, 1, nc.scalar.copy)
+
+        def read_page(s):
             for half in range(2):
                 gather(s, half * BANK, BANK)
             for half in range(2):
                 floor_at_ref(s, 2 * half, 2 * half + 2)
+
+        for s in range(1, SLICES):
+            products(s)
+            if s + 1 < SLICES:
+                feature(s + 1)
+            if s <= 2:
+                round_w1(s - 1, 1, nc.scalar.copy)
             if s == 1:
+                read_page(0)
+            scatter(s, 0, S)
+            if s > 1:
+                read_page(s - 1)
+            if s == 2:
                 quantize_w1(1, 0, 2)
-            if s == PACK - 1:
+            if s == PACK:
                 for c in range(CHUNKS):
                     weave(0, c)
-            if s == PACK:
+            if s == PACK + 1:
                 quantize_z(0, 0, CHUNKS)
-            scatter(s + 1, 0, S)
         for c in range(CHUNKS):
             calibrate(0, c)
         for step in range(CHUNKS + 3):

@@ -124,7 +124,7 @@ def tile_list_beam_slot_calibration_kernel(
 
         def round_w1(a, b, copy):
             if a == 0:
-                w1_round[b] = held.tile([P, 2 * PACK * PASS], BF16, name="w1_round", align_bytes=64)
+                w1_round[b] = held.tile([P, 2 * PACK * PASS], BF16, name="w1_round%d" % b, tag="w1_round", align_bytes=64)
                 w1_codes[b] = held.tile([P, 2 * PASS], U32, name="w1_codes%d" % b, align_bytes=64)
                 w1_planes[b] = held.tile([P, 2 * PASS], U8, name="w1_planes%d" % b, align_bytes=64)
             grouped = w1_round[b][:, a * PACK * PASS : (a + 1) * PACK * PASS]
@@ -184,13 +184,16 @@ def tile_list_beam_slot_calibration_kernel(
                     nc.scalar.activation(scaled[s][:, j0 : j0 + n], f[:], ACT.Copy, scale=gains[:, b, i : i + 1])
                 banks_f[s, j0] = f
 
-        def stage(n, name):
-            return held.tile([P, S], F32, name=name, tag="stage%d" % (n % 2))
+        def stage(tag, name):
+            return held.tile([P, S], F32, name=name, tag=tag, align_bytes=64)
+
+        def stage_of(s):
+            return "w1_round" if s % 2 else "even_stage"
 
         weighted = {}
 
         def products(s):
-            h = stage(s, "h%d" % s)
+            h = stage(stage_of(s) if s > 1 else "first", "h%d" % s)
             nc.gpsimd.tensor_tensor(h[:], scaled[s][:], cosines[s][:], ALU.mult)
             weighted[s] = ring.tile([P, S], F32, name="weighted")
             nc.gpsimd.tensor_tensor(weighted[s][:], h[:], slot_w[:], ALU.mult)
@@ -199,7 +202,7 @@ def tile_list_beam_slot_calibration_kernel(
             nc.vector.tensor_copy(pages[s % 2][:].indirect(entries(idx2, j0, n)), weighted[s][:, j0 : j0 + n])
 
         def first_slice():
-            h = stage(1, "first")
+            h = stage("first", "h0")
             weighted[0] = ring.tile([P, S], F32, name="weighted")
             head, rest = pieces(0)[0], pieces(0)[1:]
             for j0, n in pieces(0):
@@ -220,7 +223,7 @@ def tile_list_beam_slot_calibration_kernel(
 
         def gather(s, m0, n):
             if m0 == 0:
-                x_tiles[s] = stage(s + 1 if s > 0 else 0, "x%d" % s)
+                x_tiles[s] = stage(stage_of(s + 1 if s > 0 else 0), "x%d" % s)
             nc.vector.tensor_copy(x_tiles[s][:, m0 : m0 + n], pages[s % 2][:].indirect(entries(idx3, m0, n)))
 
         z_rows = [held.tile([P, CHUNKS, PACK, CHUNK], BF16, name="z_rows%d" % b) for b in range(2)]
@@ -293,17 +296,17 @@ def tile_list_beam_slot_calibration_kernel(
 
         for s in range(1, SLICES):
             products(s)
-            if s + 1 < SLICES:
-                feature(s + 1)
             if s <= 2:
                 round_w1(s - 1, 1, nc.scalar.copy)
+            if s + 1 < SLICES:
+                feature(s + 1)
             if s == 1:
                 read_page(0)
-            scatter(s, 0, S)
-            if s > 1:
-                read_page(s - 1)
             if s == 2:
                 quantize_w1(1, 0, 2)
+            scatter(s, 0, S)
+            if 1 < s < last:
+                read_page(s - 1)
             if s == PACK:
                 for c in range(CHUNKS):
                     weave(0, c)
@@ -313,9 +316,11 @@ def tile_list_beam_slot_calibration_kernel(
             calibrate(0, c)
         for step in range(CHUNKS + 3):
             if step < CHUNKS:
-                gather(last, step * CHUNK, CHUNK)
+                for s in (last - 1, last):
+                    gather(s, step * CHUNK, CHUNK)
             if 0 <= step - 1 < CHUNKS:
-                floor_at_ref(last, step - 1, step)
+                for s in (last - 1, last):
+                    floor_at_ref(s, step - 1, step)
                 weave(1, step - 1)
             if 0 <= step - 2 < CHUNKS:
                 quantize_z(1, step - 2, step - 1)

@@ -57,6 +57,9 @@ def tile_list_beam_slot_calibration_kernel(
         for page in pages:
             nc.vector.memset(page[:], 0.0)
 
+        warm = held.tile([P, 1], F32, name="warm")
+        nc.scalar.activation(warm[:], pages[0][:, 0:1], ACT.Sin)
+
 
         def load_table(a):
             words = held.tile([P, T], U32, name="tab%d" % a, align_bytes=64)

import math
from contextlib import ExitStack

import concourse.mybir as mybir

K, T, S, H, T2, M, N = 1024, 4096, 1024, 1024, 2048, 1024, 512
FLOPS = 2 * K * H * S + 2 * H * N * M

F32 = mybir.dt.float32
BF16 = mybir.dt.bfloat16
I32 = mybir.dt.int32
U32 = mybir.dt.uint32
U16 = mybir.dt.uint16
U8 = mybir.dt.uint8
FP8X4 = mybir.dt.float8_e4m3fn_x4
FP4X4 = mybir.dt.float4_e2m1fn_x4
ACT = mybir.ActivationFunctionType
ALU = mybir.AluOpType

P = 128
PACK = 4
PASS = P * PACK
BANK = 512
BANKS = 8
GROUP = 16
CHUNK = 256
CHUNKS = M // CHUNK
SLICES = H // P


def tile_list_beam_slot_calibration_kernel(
    tc, tab_words, tab_scales, offs, w1, gain, wgs, offs2, offs3, ref, w2_words, w2_scales, wm, out
):
    nc = tc.nc
    with ExitStack() as ctx:
        held = ctx.enter_context(tc.tile_pool(name="held", bufs=1))
        ring = ctx.enter_context(tc.tile_pool(name="ring", bufs=2))
        psum = ctx.enter_context(tc.psum_pool(name="psum", bufs=1))

        def entries(offsets, j0, n):
            return offsets[:, j0 // GROUP : (j0 + n) // GROUP]

        banks_taken = []

        def next_bank(shape):
            name = "bank%d" % (len(banks_taken) % BANKS)
            bank = psum.tile(shape, F32, name=name, tag=name)
            banks_taken.append(name)
            return bank

        tab_planes = held.tile([P, T], U8, name="tab_planes", align_bytes=64)
        nc.vector.memset(tab_planes[:].bitcast(I32), 0)
        w2_planes = held.tile([P, 2 * N], U8, name="w2_planes", align_bytes=64)
        nc.vector.memset(w2_planes[:].bitcast(I32), 0)

        pages = [held.tile([P, T2], F32, name="page%d" % n) for n in range(2)]
        for page in pages:
            nc.vector.memset(page[:], 0.0)

        warm = held.tile([P, 1], F32, name="warm")
        nc.scalar.activation(warm[:], pages[0][:, 0:1], ACT.Sin)


        def load_table(a):
            words = held.tile([P, T], U32, name="tab%d" % a, align_bytes=64)
            nc.sync.dma_start(
                out=words[:].bitcast(I32), in_=tab_words[a].rearrange("p t i -> p (t i)").bitcast(I32)
            )
            return words

        def load_w1(a, b):
            raw = held.tile([P, PACK, PASS], F32, name="w1_raw%d%d" % (a, b))
            rows = w1[a * PASS : (a + 1) * PASS, b * PASS : (b + 1) * PASS]
            nc.sync.dma_start(out=raw[:], in_=rows.rearrange("(p j) c -> p j c", j=PACK))
            return raw

        def load_ref(s):
            rows = held.tile([P, M], F32, name="ref%d" % s)
            nc.sync.dma_start(out=rows[:], in_=ref.rearrange("(b p i) m -> b i p m", b=2, i=PACK)[s // PACK, s % PACK])
            return rows

        table = [load_table(0)]
        idx = held.tile([P, S // GROUP], U16, name="idx")
        nc.sync.dma_start(idx[:], offs)
        for q in range(4):
            nc.sync.dma_start(
                out=tab_planes[32 * q : 32 * q + 8, :].bitcast(I32),
                in_=tab_scales[:, 4 * q : 4 * q + 4, :].bitcast(I32),
            )
        w1_raw = {(a, 0): load_w1(a, 0) for a in range(2)}
        table.append(load_table(1))
        gains = held.tile([P, 2, PACK], F32, name="gains")
        nc.sync.dma_start(out=gains[:], in_=gain.rearrange("(b p i) -> p b i", b=2, i=PACK))
        idx2 = held.tile([P, S // GROUP], U16, name="idx2")
        nc.sync.dma_start(idx2[:], offs2)
        slot_w = held.tile([P, S], F32, name="slot_w")
        nc.sync.dma_start(out=slot_w[:], in_=wgs)
        idx3 = held.tile([P, M // GROUP], U16, name="idx3")
        nc.sync.dma_start(idx3[:], offs3)
        refs = [load_ref(0)]
        for a in range(2):
            w1_raw[a, 1] = load_w1(a, 1)
        refs.extend([load_ref(s) for s in range(1, SLICES)])
        w2_codes = held.tile([P, 2, 2 * N], U8, name="w2_codes", align_bytes=64)
        nc.sync.dma_start(out=w2_codes[:].bitcast(I32), in_=w2_words.bitcast(I32).rearrange("b p c -> p b c"))
        for q in range(4):
            nc.sync.dma_start(
                out=w2_planes[32 * q : 32 * q + 4, :].bitcast(I32).rearrange("r (b c) -> r b c", b=2),
                in_=w2_scales[:, 4 * q : 4 * q + 4, :].bitcast(I32).rearrange("b r c -> r b c"),
            )
        out_w = []
        for c in range(CHUNKS):
            cols = held.tile([P, N // P, CHUNK], F32, name="out_w%d" % c)
            nc.sync.dma_start(
                out=cols[:], in_=wm[:, c * CHUNK : (c + 1) * CHUNK].rearrange("(t p) m -> p t m", p=P)
            )
            out_w.append(cols)

        picked = {}

        def pick_words(a, half):
            words = held.tile([P, BANK], U32, name="picked%d%d" % (a, half), align_bytes=64)
            nc.vector.tensor_copy(words[:], table[a][:].indirect(entries(idx, half * BANK, BANK)))
            picked[a, half] = words

        w1_round, w1_codes, w1_planes = {}, {}, {}

        def round_w1(a, b, copy):
            if a == 0:
                w1_round[b] = held.tile([P, 2 * PACK * PASS], BF16, name="w1_round%d" % b, tag="w1_round", align_bytes=64)
                w1_codes[b] = held.tile([P, 2 * PASS], U32, name="w1_codes%d" % b, align_bytes=64)
                w1_planes[b] = held.tile([P, 2 * PASS], U8, name="w1_planes%d" % b, align_bytes=64)
            grouped = w1_round[b][:, a * PACK * PASS : (a + 1) * PACK * PASS]
            copy(
                out=grouped.rearrange("p (u e m j) -> p u m j e", u=2, e=2, j=PACK),
                in_=w1_raw[a, b][:].rearrange("p j (m u e) -> p u m j e", u=2, e=2),
            )

        def quantize_w1(b, a0, a1):
            nc.vector.quantize_mx(
                out=w1_codes[b][:, a0 * PASS : a1 * PASS].bitcast(FP8X4),
                scales=w1_planes[b][:, a0 * PASS : a1 * PASS],
                in_=w1_round[b][:, a0 * PACK * PASS : a1 * PACK * PASS],
            )

        pick_words(0, 0)
        pick_words(0, 1)
        picked_planes = held.tile([P, S], U8, name="picked_planes", align_bytes=64)
        nc.vector.tensor_copy(picked_planes[:], tab_planes[:].indirect(idx[:]))
        round_w1(0, 0, nc.scalar.copy)
        round_w1(1, 0, nc.vector.tensor_copy)
        quantize_w1(0, 0, 1)
        quantize_w1(0, 1, 2)
        pick_words(1, 0)
        pick_words(1, 1)

        def pieces(s):
            if s == 0:
                return [(0, 256), (256, 256), (512, 512)]
            return [(0, BANK), (BANK, BANK)]

        banks_f, cosines, scaled = {}, {}, {}

        def feature(s):
            b, i = divmod(s, PACK)
            cosines[s] = ring.tile([P, S], F32, name="cosine")
            if s > 0:
                scaled[s] = ring.tile([P, S], F32, name="scaled")
            for j0, n in pieces(s):
                f = next_bank([P, n])
                half, c0 = divmod(j0, BANK)
                for a in range(2):
                    rows = slice(a * PASS + i * P, a * PASS + (i + 1) * P)
                    nc.tensor.matmul_mx(
                        out=f[:],
                        lhsT=w1_codes[b][:, rows].bitcast(FP8X4),
                        lhsT_scale=w1_planes[b][:, rows],
                        rhs=picked[a, half][:, c0 : c0 + n].bitcast(FP8X4),
                        rhs_scale=picked_planes[4 * a : P, j0 : j0 + n],
                        start=(a == 0),
                        stop=(a == 1),
                    )
                size = ring.tile([P, n], F32, name="size")
                nc.scalar.activation(size[:], f[:], ACT.Abs)
                nc.scalar.activation(cosines[s][:, j0 : j0 + n], size[:], ACT.Sin, scale=-1.0, bias=math.pi / 2)
                if s > 0:
                    nc.scalar.activation(scaled[s][:, j0 : j0 + n], f[:], ACT.Copy, scale=gains[:, b, i : i + 1])
                banks_f[s, j0] = f

        def stage(tag, name):
            return held.tile([P, S], F32, name=name, tag=tag, align_bytes=64)

        def stage_of(s):
            return "w1_round" if s % 2 else "even_stage"

        weighted = {}

        def products(s):
            h = stage(stage_of(s) if s > 1 else "first", "h%d" % s)
            nc.gpsimd.tensor_tensor(h[:], scaled[s][:], cosines[s][:], ALU.mult)
            weighted[s] = ring.tile([P, S], F32, name="weighted")
            nc.gpsimd.tensor_tensor(weighted[s][:], h[:], slot_w[:], ALU.mult)

        def scatter(s, j0, n):
            nc.vector.tensor_copy(pages[s % 2][:].indirect(entries(idx2, j0, n)), weighted[s][:, j0 : j0 + n])

        def first_slice():
            h = stage("first", "h0")
            weighted[0] = ring.tile([P, S], F32, name="weighted")
            head, rest = pieces(0)[0], pieces(0)[1:]
            for j0, n in pieces(0):
                cols = slice(j0, j0 + n)
                nc.vector.scalar_tensor_tensor(
                    h[:, cols], banks_f[0, j0][:], gains[:, 0, 0:1], cosines[0][:, cols], ALU.mult, ALU.mult
                )
                if (j0, n) == head:
                    nc.vector.tensor_tensor(
                        pages[0][:].indirect(entries(idx2, j0, n)), h[:, cols], slot_w[:, cols], ALU.mult
                    )
            for j0, n in rest:
                cols = slice(j0, j0 + n)
                nc.vector.tensor_tensor(weighted[0][:, cols], h[:, cols], slot_w[:, cols], ALU.mult)
            scatter(0, rest[0][0], S - rest[0][0])

        x_tiles = {}

        def gather(s, m0, n):
            if m0 == 0:
                x_tiles[s] = stage(stage_of(s + 1 if s > 0 else 0), "x%d" % s)
            nc.vector.tensor_copy(x_tiles[s][:, m0 : m0 + n], pages[s % 2][:].indirect(entries(idx3, m0, n)))

        z_rows = [held.tile([P, CHUNKS, PACK, CHUNK], BF16, name="z_rows%d" % b) for b in range(2)]

        def floor_at_ref(s, c0, c1):
            b, i = divmod(s, PACK)
            cols = slice(c0 * CHUNK, c1 * CHUNK)
            nc.vector.tensor_tensor(
                z_rows[b][:, c0:c1, i, :],
                x_tiles[s][:, cols].rearrange("p (c m) -> p c m", m=CHUNK),
                refs[s][:, cols].rearrange("p (c m) -> p c m", m=CHUNK),
                ALU.max,
            )

        z_woven, z_codes, z_planes = {}, {}, {}

        def weave(b, c):
            if c == 0:
                z_woven[b] = held.tile([P, PACK * M], BF16, name="z_woven", align_bytes=64)
                z_codes[b] = held.tile([P, M], U32, name="z_codes%d" % b, align_bytes=64)
                z_planes[b] = held.tile([P, M], U8, name="z_planes%d" % b, align_bytes=64)
            woven = z_woven[b][:, c * PACK * CHUNK : (c + 1) * PACK * CHUNK]
            nc.scalar.copy(
                out=woven.rearrange("p (g e t) -> p g t e", e=4, t=PACK),
                in_=z_rows[b][:, c, :, :].rearrange("p t (g e) -> p g t e", e=4),
            )

        def quantize_z(b, c0, c1):
            nc.vector.quantize_mx(
                out=z_codes[b][:, c0 * CHUNK : c1 * CHUNK].bitcast(FP8X4),
                scales=z_planes[b][:, c0 * CHUNK : c1 * CHUNK],
                in_=z_woven[b][:, c0 * PACK * CHUNK : c1 * PACK * CHUNK],
            )

        y_banks = {}

        def calibrate(b, c):
            for pair in range(2):
                if b == 0:
                    y_banks[c, pair] = next_bank([P, 2, CHUNK])
                for u in range(2):
                    t = 2 * pair + u
                    nc.tensor.matmul_mx(
                        out=y_banks[c, pair][:, u, :],
                        lhsT=w2_codes[:, b, 2 * P * t : 2 * P * (t + 1)].bitcast(FP4X4),
                        lhsT_scale=w2_planes[:, b * N + P * t : b * N + P * (t + 1)],
                        rhs=z_codes[b][:, c * CHUNK : (c + 1) * CHUNK].bitcast(FP8X4),
                        rhs_scale=z_planes[b][:, c * CHUNK : (c + 1) * CHUNK],
                        start=(b == 0 and u == 0),
                        stop=(b == 1 and u == 1),
                    )

        def weigh(c):
            for pair in range(2):
                both = out_w[c][:, 2 * pair : 2 * pair + 2, :]
                nc.vector.tensor_tensor(both, y_banks[c, pair][:], both, ALU.mult)
                rows = out[2 * P * pair : 2 * P * (pair + 1), c * CHUNK : (c + 1) * CHUNK]
                nc.sync.dma_start(out=rows.rearrange("(u p) m -> p u m", p=P), in_=both)

        feature(0)
        feature(1)
        first_slice()
        last = SLICES - 1

        def read_page(s):
            for half in range(2):
                gather(s, half * BANK, BANK)
            for half in range(2):
                floor_at_ref(s, 2 * half, 2 * half + 2)

        for s in range(1, SLICES):
            products(s)
            if s <= 2:
                round_w1(s - 1, 1, nc.scalar.copy)
            if s + 1 < SLICES:
                feature(s + 1)
            if s == 1:
                read_page(0)
            if s == 2:
                quantize_w1(1, 0, 2)
            scatter(s, 0, S)
            if 1 < s < last:
                read_page(s - 1)
            if s == PACK:
                for c in range(CHUNKS):
                    weave(0, c)
            if s == PACK + 1:
                quantize_z(0, 0, CHUNKS)
        for c in range(CHUNKS):
            calibrate(0, c)
        for step in range(CHUNKS + 3):
            if step < CHUNKS:
                for s in (last - 1, last):
                    gather(s, step * CHUNK, CHUNK)
            if 0 <= step - 1 < CHUNKS:
                for s in (last - 1, last):
                    floor_at_ref(s, step - 1, step)
                weave(1, step - 1)
            if 0 <= step - 2 < CHUNKS:
                quantize_z(1, step - 2, step - 1)
                calibrate(1, step - 2)
            if 0 <= step - 3 < CHUNKS:
                weigh(step - 3)
